import numpy as np, ml_dtypes
CORES = [1,129,9,137,57,185,105,233,113,241,121,249]
N = 12
import mx_ref
NC, KB = 256, 1
BF = ml_dtypes.bfloat16
def cut(t, i, w=512):
    return t[:, w * i:w * i + w]
def term(a, B):
    return np.stack([mx_ref.matmul(mx_ref.quantize(cut(a, i)), B) for i in range(4)], axis=2).reshape(128, -1)
def setup_inputs(rng):
    def f(*shape):
        return mx_ref.flush((rng.standard_normal(shape, dtype=np.float32) * np.exp2(rng.integers(-2, 3, shape[:-1] + (1,)))).astype(BF))
    return {"a": f(N, 128, 4 * 512), "b": f(N, 128, KB * 4 * NC)}
def setup_inputs_blocks(rng):
    d = setup_inputs(rng)
    for k in ("a", "b"): d[k] = mx_ref.spread(d[k], rng, 2)
    return d
def setup_inputs_wide(rng):
    d = setup_inputs(rng)
    for k in ("a", "b"): d[k] = mx_ref.flush((d[k].astype(np.float32) * np.exp2(rng.integers(-4, 5, (N, 1, 1))).astype(np.float32)).astype(BF))
    return d
def setup_inputs_lossless(rng):
    a = np.zeros((N, 128, 4 * 128, 4), np.float32)
    for r in range(N):
        k = rng.integers(0, 512, size=4 * 128)
        a[r, k // 4, np.arange(4 * 128), k % 4] = 1.0
    size = np.repeat(2.0 ** rng.integers(-4, 5, size=(1, 1, (KB * 4 * NC) // 4)), 4, axis=2)
    b = rng.integers(-1, 2, size=(N, 128, KB * 4 * NC)) * size
    return {"a": a.reshape(N, 128, 4 * 512).astype(BF), "b": b.astype(np.float32).astype(BF)}
def reference(a, b):
    y = np.zeros((N, 128, KB * 4 * NC), np.float32)
    for k in range(KB):
        y[:, :, 4 * NC * k:4 * NC * k + 4 * NC] = mx_ref.total([term(a[r], mx_ref.quantize(cut(b[r], k, 4 * NC))) for r in range(N)])
    return {"y": y}

@@ -1,0 +1,288 @@
+from concourse.bass import DstId, RemoteDMATransfer
+from concourse.mybir import dt, AluOpType, ActivationFunctionType
+
+K = 4
+SLOT = 192
+
+SCRATCH = {
+    "a_sb": ("sbuf", [128, 2048], "bfloat16"),
+    "b_sb": ("sbuf", [128, 1024], "bfloat16"),
+    "aq": ("sbuf", [128, 512], "float8_e4m3fn_x4"), "ax": ("sbuf", [128, 512], "uint8"),
+    "bq": ("sbuf", [128, 256], "float8_e4m3fn_x4"), "bx": ("sbuf", [128, 256], "uint8"),
+    "t_bf": ("sbuf", [128, 1024], "bfloat16"),
+    "tq": ("sbuf", [128, 256], "float8_e4m3fn_x4"), "tx": ("sbuf", [128, 256], "uint8"),
+    "yc": ("sbuf", [128, 256], "float8_e4m3fn_x4"), "yx": ("sbuf", [128, 256], "uint8"),
+    "y_sb": ("sbuf", [128, 1024], "float32"),
+    "dg": ("sbuf", [128, 520], "bfloat16"),
+    "idc": ("sbuf", [128, 512], "float8_e4m3fn_x4"), "idx": ("sbuf", [128, 512], "uint8"),
+    "zb": ("sbuf", [128, 512], "bfloat16"),
+    "pt1": ("sbuf", [128, 512], "bfloat16"), "pt2": ("sbuf", [128, 512], "bfloat16"),
+    "pq1": ("sbuf", [128, 128], "float8_e4m3fn_x4"), "px1": ("sbuf", [128, 128], "uint8"),
+    "pq2": ("sbuf", [128, 128], "float8_e4m3fn_x4"), "px2": ("sbuf", [128, 128], "uint8"),
+    "lc": ("sbuf", [128, 7 * SLOT], "float8_e4m3fn_x4"), "lx": ("sbuf", [128, 7 * SLOT], "uint8"),
+    "ps": ("psum", [128, 4096], "float32"),
+}
+SEMAPHORES = (["ones", "diag", "idq", "zz", "pad", "sent", "idin", "ld_b", "qb", "q1", "q2",
+               "c1v", "c1s", "c2v", "c2s", "tq0", "tq1", "y0", "y1", "ov0", "ov1", "os0", "os1", "st0", "st1"]
+              + ["ld_a%d" % i for i in range(4)] + ["qa%d" % i for i in range(4)] + ["mm%d" % i for i in range(4)]
+              + ["cs%d" % i for i in range(4)] + ["l1_%d" % i for i in range(4)] + ["l2_%d" % i for i in range(3)]
+              + ["p1_%d" % i for i in range(4)] + ["p2_%d" % i for i in range(4)]
+              + ["u%d_%d" % (h, i) for h in range(2) for i in range(4)])
+
+_CACHE = {}
+
+
+def _bits(m):
+    return bin(m).count("1")
+
+
+def _same_chip(topo, a, b):
+    return topo.host(a) == topo.host(b) and topo.chip(a) == topo.chip(b)
+
+
+def _plan(T, topo):
+    if "p" in _CACHE:
+        return _CACHE["p"]
+    cores = [int(c) for c in T.cores]
+    hosts = sorted(set(topo.host(c) for c in cores))
+    world = range((max(hosts) + 1) * topo.CORES_PER_HOST)
+    planes = []
+    for c in cores:
+        for pl in planes:
+            if topo.same_plane(pl[0], c):
+                pl.append(c)
+                break
+        else:
+            planes.append([c])
+    planes.sort(key=len)
+    minor_all, major_all = planes
+
+    def helpers(c, other):
+        return [d for d in world if d != c and _same_chip(topo, d, c) and topo.die(d) == topo.die(c)
+                and topo.may_write(d, other)]
+
+    major = [[c for c in major_all if topo.host(c) == h] for h in hosts]
+    minor = [[c for c in minor_all if topo.host(c) == h] for h in hosts]
+    per = K // len(minor[0])
+    F = [[helpers(major[h][q], minor[h][0])[0] for q in range(K)] for h in range(len(hosts))]
+    E = [[helpers(minor[h][q // per], major[h][0])[q % per] for q in range(K)] for h in range(len(hosts))]
+    role = {}
+    for h in range(len(hosts)):
+        for k, c in enumerate(major[h]):
+            role[c] = ("rank", h, k, F[h], k, 1)
+        for k, c in enumerate(minor[h]):
+            role[c] = ("rank", h, k, E[h], K + k, per)
+        for q in range(K):
+            role[F[h][q]] = ("F", h, q)
+            role[E[h][q]] = ("E", h, q)
+    p = {"major": major, "minor": minor, "F": F, "E": E, "role": role, "per": per}
+    _CACHE["p"] = p
+    return p
+
+
+def _u8(view):
+    return view.bitcast(dt.uint8)
+
+
+def _send(g, T, topo, core, dst, sem, mask, out_c, in_c, out_x, in_x, sent):
+    rid, pid = topo.addr(dst, core)
+    g.remote_dma(out_ap=out_x, in_ap=in_x, remote_sem=sem, local_sem=T.sem.sent, pid=pid, routing_id=rid,
+                 dma_engine_mask=mask)
+    g.remote_dma(out_ap=_u8(out_c), in_ap=_u8(in_c), remote_sem=sem, local_sem=T.sem.sent, pid=pid, routing_id=rid,
+                 dma_engine_mask=mask)
+    sent[0] += 2 * _bits(mask)
+
+
+def _send_many(g, T, topo, core, dsts, sem, mask, out_c, in_c, out_x, in_x, sent):
+    ids = []
+    for d in dsts:
+        rid, pid = topo.addr(d, core)
+        ids.append(DstId(rid=rid, pnc=pid))
+    g.remote_dma_fused([RemoteDMATransfer(dst_ids=ids, dma_engine_mask=mask, remote_sem=sem, srcs=[in_x],
+                                          dsts=[out_x for _ in dsts])], local_sem=T.sem.sent)
+    g.remote_dma_fused([RemoteDMATransfer(dst_ids=ids, dma_engine_mask=mask, remote_sem=sem, srcs=[_u8(in_c)],
+                                          dsts=[_u8(out_c) for _ in dsts])], local_sem=T.sem.sent)
+    sent[0] += 2 * _bits(mask)
+
+
+def _masks(topo, core, near, far):
+    off = topo.mask(core, far)
+    return off, topo.mask(core, near) & ~off
+
+
+def _sel(T, i):
+    return T.idc[:, 128 * i:128 * i + 128], T.idx[:, 128 * i:128 * i + 128]
+
+
+def _rank(g, core, T, topo, P, h, k, owners, d_index, n_id):
+    v, t, s, sy, S = g.vector, g.tensor, g.scalar, g.sync, T.sem
+    w = 256 // K
+    sent = [0]
+    sy.dma_start(T.b_sb[:], T.b[:]).then_inc(S.ld_b, 16)
+    for i in range(4):
+        (s if i % 2 == 0 else sy).dma_start(T.a_sb[:, 512 * i:512 * i + 512],
+                                            T.a[:, 512 * i:512 * i + 512]).then_inc(S["ld_a%d" % i], 16)
+    v.wait_ge(S.ld_b, 16)
+    v.quantize_mx(T.bq[:], T.bx[:], T.b_sb[:]).then_inc(S.qb, 1)
+    t.wait_ge(S.qb, 1)
+    for i in range(4):
+        v.wait_ge(S["ld_a%d" % i], 16)
+        v.quantize_mx(T.aq[:, 128 * i:128 * i + 128], T.ax[:, 128 * i:128 * i + 128],
+                      T.a_sb[:, 512 * i:512 * i + 512]).then_inc(S["qa%d" % i], 1)
+        t.wait_ge(S["qa%d" % i], 1)
+        t.matmul_mx(T.ps[:, 512 * i:512 * i + 256], T.aq[:, 128 * i:128 * i + 128], T.ax[:, 128 * i:128 * i + 128],
+                    T.bq[:], T.bx[:], True, True).then_inc(S["mm%d" % i], 1)
+    for i in range(3):
+        s.wait_ge(S["mm%d" % i], 1)
+        s.activation(T.t_bf[:, i:1024:4], T.ps[:, 512 * i:512 * i + 256],
+                     ActivationFunctionType.Copy).then_inc(S["cs%d" % i], 1)
+    v.wait_ge(S.mm3, 1)
+    v.tensor_copy(T.t_bf[:, 3:1024:4], T.ps[:, 1536:1792]).then_inc(S.cs3, 1)
+    far = [q for q in range(K) if not _same_chip(topo, owners[q], core)]
+    near = [q for q in range(K) if _same_chip(topo, owners[q], core)]
+    far = [q for q in far if q > near[-1]] + [q for q in far if q < near[0]]
+    halves = [far[0] // 2, 1 - far[0] // 2]
+    for i in range(4):
+        v.wait_ge(S["cs%d" % i], 1)
+    for H in halves:
+        v.quantize_mx(T.tq[:, 128 * H:128 * H + 128], T.tx[:, 128 * H:128 * H + 128],
+                      T.t_bf[:, 512 * H:512 * H + 512]).then_inc(S["tq%d" % H], 1)
+    off, on = _masks(topo, core, owners[near[0]], owners[far[0]])
+    seen = set()
+    for q in far + near:
+        if q // 2 not in seen:
+            g.wait_ge(S["tq%d" % (q // 2)], 1)
+            seen.add(q // 2)
+        _send(g, T, topo, core, owners[q], S["l1_%d" % k], off if q in far else on,
+              T.lc[:, SLOT * k:SLOT * k + w], T.tq[:, w * q:w * q + w],
+              T.lx[:, SLOT * k:SLOT * k + w], T.tx[:, w * q:w * q + w], sent)
+    n_r = len(P["major"][h]) + len(P["minor"][h])
+    due = [max((d_index - q - 1) % n_r if q != d_index else -1 for q in (2 * H, 2 * H + 1)) for H in range(2)]
+    order = [0, 1] if due[0] <= due[1] else [1, 0]
+    t.wait_ge(S.idin, n_id * 2 * _bits(off))
+    for n, H in enumerate(order):
+        if n == 1:
+            for i in range(4):
+                t.wait_ge(S["cs%d" % i], 1)
+        t.wait_ge(S["y%d" % H], 4 * _bits(off))
+        for i in range(4):
+            bank = 512 * (i + 4 * (1 - n))
+            c, x = _sel(T, i)
+            t.matmul_mx(T.ps[:, bank:bank + 128], c, x, T.yc[:, 128 * H:128 * H + 128],
+                        T.yx[:, 128 * H:128 * H + 128], True, True).then_inc(S["u%d_%d" % (H, i)], 1)
+        for i in range(4):
+            bank = 512 * (i + 4 * (1 - n))
+            out = T.y_sb[:, 512 * H + i:512 * H + 512:4]
+            if i < 2:
+                v.wait_ge(S["u%d_%d" % (H, i)], 1)
+                v.tensor_copy(out, T.ps[:, bank:bank + 128]).then_inc(S["ov%d" % H], 1)
+            else:
+                s.wait_ge(S["u%d_%d" % (H, i)], 1)
+                s.activation(out, T.ps[:, bank:bank + 128], ActivationFunctionType.Copy).then_inc(S["os%d" % H], 1)
+        sy.wait_ge(S["ov%d" % H], 2)
+        sy.wait_ge(S["os%d" % H], 2)
+        sy.dma_start(T.y[:, 512 * H:512 * H + 512], T.y_sb[:, 512 * H:512 * H + 512]).then_inc(S["st%d" % H], 16)
+    for H in order:
+        sy.wait_ge(S["st%d" % H], 16)
+    g.wait_ge(S.sent, sent[0])
+
+
+def _add(g, T, sources, first_bank, tile, done, cv, cs):
+    v, t, s, S = g.vector, g.tensor, g.scalar, T.sem
+    w = 256 // K
+    for n, (sem, cnt, c, x) in enumerate(sources):
+        t.wait_ge(sem, cnt)
+        for i in range(4):
+            bank = 512 * (first_bank + i)
+            ic, ix = _sel(T, i)
+            mm = t.matmul_mx(T.ps[:, bank:bank + 128], ic, ix, c, x, n == 0, n == len(sources) - 1)
+            if n == len(sources) - 1:
+                mm.then_inc(S["%s_%d" % (done, i)], 1)
+    for i in range(4):
+        bank = 512 * (first_bank + i)
+        if i < 2:
+            v.wait_ge(S["%s_%d" % (done, i)], 1)
+            v.tensor_copy(tile[:, i:4 * w:4], T.ps[:, bank:bank + w]).then_inc(cv, 1)
+        else:
+            s.wait_ge(S["%s_%d" % (done, i)], 1)
+            s.activation(tile[:, i:4 * w:4], T.ps[:, bank:bank + w], ActivationFunctionType.Copy).then_inc(cs, 1)
+    v.wait_ge(cv, 2)
+    v.wait_ge(cs, 2)
+
+
+def _helper(g, core, T, topo, P, kind, h, q):
+    v, t, S = g.vector, g.tensor, T.sem
+    w = 256 // K
+    sent = [0]
+    final = kind == "F"
+    per = P["per"]
+    my_rank = P["major"][h][q] if final else P["minor"][h][q // per]
+    twin = P["F"][1 - h][q]
+    off, on = _masks(topo, core, my_rank, twin)
+    ne = _bits(off)
+    slots = list(range(7)) if final else list(range(len(P["minor"][h])))
+    v.memset(T.dg[:, 0:516], 1.0).then_inc(S.ones, 1)
+    v.memset(T.zb[:], 0.0).then_inc(S.zz, 1)
+    v.memset(T.pt1[:, 4 * w:512], 0.0).then_inc(S.zz, 1)
+    v.memset(T.pt2[:, 4 * w:512], 0.0).then_inc(S.zz, 1)
+    g.wait_ge(S.ones, 1)
+    g.affine_select(T.dg[:, 0:516], T.dg[:, 0:516], [[1, 516]], AluOpType.is_equal, 0.0, -3, -4).then_inc(S.diag, 1)
+    v.wait_ge(S.diag, 1)
+    for i in range(4):
+        c, x = _sel(T, i)
+        v.quantize_mx(c, x, T.dg[:, 3 - i:515 - i]).then_inc(S.idq, 1)
+    v.wait_ge(S.zz, 3)
+    for sl in slots:
+        v.quantize_mx(T.lc[:, SLOT * sl + w:SLOT * sl + SLOT], T.lx[:, SLOT * sl + w:SLOT * sl + SLOT],
+                      T.zb[:]).then_inc(S.pad, 1)
+    g.wait_ge(S.idq, 4)
+    share = 512 if final else 512 // per
+    lo = 0 if final else share * (q % per)
+    _send(g, T, topo, core, my_rank, S.idin, off, T.idc[:, lo:lo + share], T.idc[:, lo:lo + share],
+          T.idx[:, lo:lo + share], T.idx[:, lo:lo + share], sent)
+    t.wait_ge(S.idq, 4)
+    t.wait_ge(S.pad, len(slots))
+
+    def slot(sl):
+        return T.lc[:, SLOT * sl:SLOT * sl + 128], T.lx[:, SLOT * sl:SLOT * sl + 128]
+
+    if final:
+        order = [(q - 1) % K, (q - 2) % K, q, (q - 3) % K]
+    else:
+        mine, other = q // per, 1 - q // per
+        order = [other, mine] if q % per == 0 else [mine, other]
+    _add(g, T, [(S["l1_%d" % k], 2 * ne) + slot(k) for k in order], 0, T.pt1, "p1", S.c1v, S.c1s)
+    v.quantize_mx(T.pq1[:], T.px1[:], T.pt1[:]).then_inc(S.q1, 1)
+    g.wait_ge(S.q1, 1)
+    if not final:
+        sl = K + h
+        _send_many(g, T, topo, core, [P["F"][h][q], twin], S["l2_%d" % h], off,
+                   T.lc[:, SLOT * sl:SLOT * sl + w], T.pq1[:, 0:w], T.lx[:, SLOT * sl:SLOT * sl + w], T.px1[:, 0:w], sent)
+        g.wait_ge(S.sent, sent[0])
+        return
+    sl = K + 2
+    _send(g, T, topo, core, twin, S.l2_2, off, T.lc[:, SLOT * sl:SLOT * sl + w], T.pq1[:, 0:w],
+          T.lx[:, SLOT * sl:SLOT * sl + w], T.px1[:, 0:w], sent)
+    src = [(S.q1, 1, T.pq1[:], T.px1[:])]
+    for j in (h, 2, 1 - h):
+        src.append((S["l2_%d" % j], 2 * ne) + slot(K + j))
+    _add(g, T, src, 4, T.pt2, "p2", S.c2v, S.c2s)
+    v.quantize_mx(T.pq2[:], T.px2[:], T.pt2[:]).then_inc(S.q2, 1)
+    g.wait_ge(S.q2, 1)
+    ranks = P["major"][h] + P["minor"][h]
+    away = [ranks[(q + 1 + n) % len(ranks)] for n in range(len(ranks) - 1)]
+    oc, ox = T.yc[:, w * q:w * q + w], T.yx[:, w * q:w * q + w]
+    _send_many(g, T, topo, core, away, S["y%d" % (q // 2)], off, oc, T.pq2[:, 0:w], ox, T.px2[:, 0:w], sent)
+    _send(g, T, topo, core, my_rank, S["y%d" % (q // 2)], on, oc, T.pq2[:, 0:w], ox, T.px2[:, 0:w], sent)
+    g.wait_ge(S.sent, sent[0])
+
+
+def rank_program(g, core, T, topo):
+    P = _plan(T, topo)
+    r = P["role"].get(core)
+    if r is None:
+        return
+    if r[0] == "rank":
+        _rank(g, core, T, topo, P, r[1], r[2], r[3], r[4], r[5])
+    else:
+        _helper(g, core, T, topo, P, r[0], r[1], r[2])

@@ -16,13 +16,14 @@ SCRATCH = {
     "dg": ("sbuf", [128, 520], "bfloat16"),
     "idc": ("sbuf", [128, 512], "float8_e4m3fn_x4"), "idx": ("sbuf", [128, 512], "uint8"),
     "zb": ("sbuf", [128, 512], "bfloat16"),
+    "zq": ("sbuf", [128, 128], "float8_e4m3fn_x4"), "zx": ("sbuf", [128, 128], "uint8"),
     "pt1": ("sbuf", [128, 512], "bfloat16"), "pt2": ("sbuf", [128, 512], "bfloat16"),
     "pq1": ("sbuf", [128, 128], "float8_e4m3fn_x4"), "px1": ("sbuf", [128, 128], "uint8"),
     "pq2": ("sbuf", [128, 128], "float8_e4m3fn_x4"), "px2": ("sbuf", [128, 128], "uint8"),
     "lc": ("sbuf", [128, 7 * SLOT], "float8_e4m3fn_x4"), "lx": ("sbuf", [128, 7 * SLOT], "uint8"),
     "ps": ("psum", [128, 4096], "float32"),
 }
-SEMAPHORES = (["ones", "diag", "idq", "zz", "pad", "sent", "idin", "ld_b", "qb", "q1", "q2",
+SEMAPHORES = (["ones", "diag", "idq", "zz", "pad", "padin", "mm3b", "cs3b", "sent", "idin", "ld_b", "qb", "q1", "q2",
                "c1v", "c1s", "c2v", "c2s", "tq0", "tq1", "y0", "y1", "ov0", "ov1", "os0", "os1", "st0", "st1"]
               + ["ld_a%d" % i for i in range(4)] + ["qa%d" % i for i in range(4)] + ["mm%d" % i for i in range(4)]
               + ["cs%d" % i for i in range(4)] + ["l1_%d" % i for i in range(4)] + ["l2_%d" % i for i in range(3)]
@@ -110,6 +111,10 @@ def _masks(topo, core, near, far):
     return off, topo.mask(core, near) & ~off
 
 
+def _group(d):
+    return d // (K // 2) if d < K else (d - K) % 2
+
+
 def _sel(T, i):
     return T.idc[:, 128 * i:128 * i + 128], T.idx[:, 128 * i:128 * i + 128]
 
@@ -118,10 +123,22 @@ def _rank(g, core, T, topo, P, h, k, owners, d_index, n_id):
     v, t, s, sy, S = g.vector, g.tensor, g.scalar, g.sync, T.sem
     w = 256 // K
     sent = [0]
+    far = [q for q in range(K) if not _same_chip(topo, owners[q], core)]
+    near = [q for q in range(K) if _same_chip(topo, owners[q], core)]
+    far = [q for q in far if q > near[-1]] + [q for q in far if q < near[0]]
+    halves = [far[0] // 2, 1 - far[0] // 2]
     sy.dma_start(T.b_sb[:], T.b[:]).then_inc(S.ld_b, 16)
     for i in range(4):
         (s if i % 2 == 0 else sy).dma_start(T.a_sb[:, 512 * i:512 * i + 512],
                                             T.a[:, 512 * i:512 * i + 512]).then_inc(S["ld_a%d" % i], 16)
+    v.memset(T.zb[:], 0.0).then_inc(S.zz, 1)
+    v.wait_ge(S.zz, 1)
+    v.quantize_mx(T.zq[:], T.zx[:], T.zb[:]).then_inc(S.pad, 1)
+    g.wait_ge(S.pad, 1)
+    full = topo.mask(core, owners[near[0]])
+    for q in near:
+        _send(g, T, topo, core, owners[q], S.padin, full, T.lc[:, SLOT * k + w:SLOT * k + 2 * w], T.zq[:, 0:w],
+              T.lx[:, SLOT * k + w:SLOT * k + 2 * w], T.zx[:, 0:w], sent)
     v.wait_ge(S.ld_b, 16)
     v.quantize_mx(T.bq[:], T.bx[:], T.b_sb[:]).then_inc(S.qb, 1)
     t.wait_ge(S.qb, 1)
@@ -130,21 +147,25 @@ def _rank(g, core, T, topo, P, h, k, owners, d_index, n_id):
         v.quantize_mx(T.aq[:, 128 * i:128 * i + 128], T.ax[:, 128 * i:128 * i + 128],
                       T.a_sb[:, 512 * i:512 * i + 512]).then_inc(S["qa%d" % i], 1)
         t.wait_ge(S["qa%d" % i], 1)
-        t.matmul_mx(T.ps[:, 512 * i:512 * i + 256], T.aq[:, 128 * i:128 * i + 128], T.ax[:, 128 * i:128 * i + 128],
-                    T.bq[:], T.bx[:], True, True).then_inc(S["mm%d" % i], 1)
+        if i < 3:
+            t.matmul_mx(T.ps[:, 512 * i:512 * i + 256], T.aq[:, 128 * i:128 * i + 128], T.ax[:, 128 * i:128 * i + 128],
+                        T.bq[:], T.bx[:], True, True).then_inc(S["mm%d" % i], 1)
+    for n, H in enumerate(halves):
+        t.matmul_mx(T.ps[:, 512 * (3 + n):512 * (3 + n) + 128], T.aq[:, 384:512], T.ax[:, 384:512],
+                    T.bq[:, 128 * H:128 * H + 128], T.bx[:, 128 * H:128 * H + 128],
+                    True, True).then_inc(S["mm3" if n == 0 else "mm3b"], 1)
     for i in range(3):
         s.wait_ge(S["mm%d" % i], 1)
         s.activation(T.t_bf[:, i:1024:4], T.ps[:, 512 * i:512 * i + 256],
                      ActivationFunctionType.Copy).then_inc(S["cs%d" % i], 1)
-    v.wait_ge(S.mm3, 1)
-    v.tensor_copy(T.t_bf[:, 3:1024:4], T.ps[:, 1536:1792]).then_inc(S.cs3, 1)
-    far = [q for q in range(K) if not _same_chip(topo, owners[q], core)]
-    near = [q for q in range(K) if _same_chip(topo, owners[q], core)]
-    far = [q for q in far if q > near[-1]] + [q for q in far if q < near[0]]
-    halves = [far[0] // 2, 1 - far[0] // 2]
-    for i in range(4):
-        v.wait_ge(S["cs%d" % i], 1)
-    for H in halves:
+    for n, H in enumerate(halves):
+        v.wait_ge(S["mm3" if n == 0 else "mm3b"], 1)
+        v.tensor_copy(T.t_bf[:, 512 * H + 3:512 * H + 512:4],
+                      T.ps[:, 512 * (3 + n):512 * (3 + n) + 128]).then_inc(S["cs3" if n == 0 else "cs3b"], 1)
+        if n == 0:
+            for i in range(3):
+                v.wait_ge(S["cs%d" % i], 1)
+        v.wait_ge(S["cs3" if n == 0 else "cs3b"], 1)
         v.quantize_mx(T.tq[:, 128 * H:128 * H + 128], T.tx[:, 128 * H:128 * H + 128],
                       T.t_bf[:, 512 * H:512 * H + 512]).then_inc(S["tq%d" % H], 1)
     off, on = _masks(topo, core, owners[near[0]], owners[far[0]])
@@ -156,10 +177,10 @@ def _rank(g, core, T, topo, P, h, k, owners, d_index, n_id):
         _send(g, T, topo, core, owners[q], S["l1_%d" % k], off if q in far else on,
               T.lc[:, SLOT * k:SLOT * k + w], T.tq[:, w * q:w * q + w],
               T.lx[:, SLOT * k:SLOT * k + w], T.tx[:, w * q:w * q + w], sent)
-    n_r = len(P["major"][h]) + len(P["minor"][h])
-    due = [max((d_index - q - 1) % n_r if q != d_index else -1 for q in (2 * H, 2 * H + 1)) for H in range(2)]
-    order = [0, 1] if due[0] <= due[1] else [1, 0]
-    t.wait_ge(S.idin, n_id * 2 * _bits(off))
+    first = _group(d_index)
+    order = [first, 1 - first]
+    t.wait_ge(S.idin, n_id * 2 * _bits(full))
+    t.wait_ge(S.cs3b, 1)
     for n, H in enumerate(order):
         if n == 1:
             for i in range(4):
@@ -232,16 +253,19 @@ def _helper(g, core, T, topo, P, kind, h, q):
         c, x = _sel(T, i)
         v.quantize_mx(c, x, T.dg[:, 3 - i:515 - i]).then_inc(S.idq, 1)
     v.wait_ge(S.zz, 3)
-    for sl in slots:
+    own = q if final else q // per
+    for sl in [x for x in slots if x != own]:
         v.quantize_mx(T.lc[:, SLOT * sl + w:SLOT * sl + SLOT], T.lx[:, SLOT * sl + w:SLOT * sl + SLOT],
                       T.zb[:]).then_inc(S.pad, 1)
     g.wait_ge(S.idq, 4)
     share = 512 if final else 512 // per
     lo = 0 if final else share * (q % per)
-    _send(g, T, topo, core, my_rank, S.idin, off, T.idc[:, lo:lo + share], T.idc[:, lo:lo + share],
+    full = topo.mask(core, my_rank)
+    _send(g, T, topo, core, my_rank, S.idin, full, T.idc[:, lo:lo + share], T.idc[:, lo:lo + share],
           T.idx[:, lo:lo + share], T.idx[:, lo:lo + share], sent)
     t.wait_ge(S.idq, 4)
-    t.wait_ge(S.pad, len(slots))
+    t.wait_ge(S.pad, len(slots) - 1)
+    t.wait_ge(S.padin, 2 * _bits(full))
 
     def slot(sl):
         return T.lc[:, SLOT * sl:SLOT * sl + 128], T.lx[:, SLOT * sl:SLOT * sl + 128]
@@ -270,10 +294,15 @@ def _helper(g, core, T, topo, P, kind, h, q):
     v.quantize_mx(T.pq2[:], T.px2[:], T.pt2[:]).then_inc(S.q2, 1)
     g.wait_ge(S.q2, 1)
     ranks = P["major"][h] + P["minor"][h]
-    away = [ranks[(q + 1 + n) % len(ranks)] for n in range(len(ranks) - 1)]
+    mine = _group(q)
+    r1 = [c for d, c in enumerate(ranks) if _group(d) == mine and c != my_rank]
+    r2 = [c for d, c in enumerate(ranks) if _group(d) != mine]
+    rot = q % 2
+    r1, r2 = r1[rot:] + r1[:rot], r2[rot:] + r2[:rot]
     oc, ox = T.yc[:, w * q:w * q + w], T.yx[:, w * q:w * q + w]
-    _send_many(g, T, topo, core, away, S["y%d" % (q // 2)], off, oc, T.pq2[:, 0:w], ox, T.px2[:, 0:w], sent)
-    _send(g, T, topo, core, my_rank, S["y%d" % (q // 2)], on, oc, T.pq2[:, 0:w], ox, T.px2[:, 0:w], sent)
+    _send_many(g, T, topo, core, r1, S["y%d" % mine], off, oc, T.pq2[:, 0:w], ox, T.px2[:, 0:w], sent)
+    _send(g, T, topo, core, my_rank, S["y%d" % mine], on, oc, T.pq2[:, 0:w], ox, T.px2[:, 0:w], sent)
+    _send_many(g, T, topo, core, r2, S["y%d" % mine], off, oc, T.pq2[:, 0:w], ox, T.px2[:, 0:w], sent)
     g.wait_ge(S.sent, sent[0])
 
 

from concourse.bass import DstId, RemoteDMATransfer
from concourse.mybir import dt, AluOpType, ActivationFunctionType

K = 4
SLOT = 192

SCRATCH = {
    "a_sb": ("sbuf", [128, 2048], "bfloat16"),
    "b_sb": ("sbuf", [128, 1024], "bfloat16"),
    "aq": ("sbuf", [128, 512], "float8_e4m3fn_x4"), "ax": ("sbuf", [128, 512], "uint8"),
    "bq": ("sbuf", [128, 256], "float8_e4m3fn_x4"), "bx": ("sbuf", [128, 256], "uint8"),
    "t_bf": ("sbuf", [128, 1024], "bfloat16"),
    "tq": ("sbuf", [128, 256], "float8_e4m3fn_x4"), "tx": ("sbuf", [128, 256], "uint8"),
    "yc": ("sbuf", [128, 256], "float8_e4m3fn_x4"), "yx": ("sbuf", [128, 256], "uint8"),
    "y_sb": ("sbuf", [128, 1024], "float32"),
    "dg": ("sbuf", [128, 520], "bfloat16"),
    "idc": ("sbuf", [128, 512], "float8_e4m3fn_x4"), "idx": ("sbuf", [128, 512], "uint8"),
    "zb": ("sbuf", [128, 512], "bfloat16"),
    "zq": ("sbuf", [128, 128], "float8_e4m3fn_x4"), "zx": ("sbuf", [128, 128], "uint8"),
    "pt1": ("sbuf", [128, 512], "bfloat16"), "pt2": ("sbuf", [128, 512], "bfloat16"),
    "pq1": ("sbuf", [128, 128], "float8_e4m3fn_x4"), "px1": ("sbuf", [128, 128], "uint8"),
    "pq2": ("sbuf", [128, 128], "float8_e4m3fn_x4"), "px2": ("sbuf", [128, 128], "uint8"),
    "lc": ("sbuf", [128, 7 * SLOT], "float8_e4m3fn_x4"), "lx": ("sbuf", [128, 7 * SLOT], "uint8"),
    "ps": ("psum", [128, 4096], "float32"),
}
SEMAPHORES = (["ones", "diag", "idq", "zz", "pad", "padin", "mm3b", "cs3b", "sent", "idin", "ld_b", "qb", "q1", "q2",
               "c1v", "c1s", "c2v", "c2s", "tq0", "tq1", "y0", "y1", "ov0", "ov1", "os0", "os1", "st0", "st1"]
              + ["ld_a%d" % i for i in range(4)] + ["qa%d" % i for i in range(4)] + ["mm%d" % i for i in range(4)]
              + ["cs%d" % i for i in range(4)] + ["l1_%d" % i for i in range(4)] + ["l2_%d" % i for i in range(3)]
              + ["p1_%d" % i for i in range(4)] + ["p2_%d" % i for i in range(4)]
              + ["u%d_%d" % (h, i) for h in range(2) for i in range(4)])

_CACHE = {}


def _bits(m):
    return bin(m).count("1")


def _same_chip(topo, a, b):
    return topo.host(a) == topo.host(b) and topo.chip(a) == topo.chip(b)


def _plan(T, topo):
    if "p" in _CACHE:
        return _CACHE["p"]
    cores = [int(c) for c in T.cores]
    hosts = sorted(set(topo.host(c) for c in cores))
    world = range((max(hosts) + 1) * topo.CORES_PER_HOST)
    planes = []
    for c in cores:
        for pl in planes:
            if topo.same_plane(pl[0], c):
                pl.append(c)
                break
        else:
            planes.append([c])
    planes.sort(key=len)
    minor_all, major_all = planes

    def helpers(c, other):
        return [d for d in world if d != c and _same_chip(topo, d, c) and topo.die(d) == topo.die(c)
                and topo.may_write(d, other)]

    major = [[c for c in major_all if topo.host(c) == h] for h in hosts]
    minor = [[c for c in minor_all if topo.host(c) == h] for h in hosts]
    per = K // len(minor[0])
    F = [[helpers(major[h][q], minor[h][0])[0] for q in range(K)] for h in range(len(hosts))]
    E = [[helpers(minor[h][q // per], major[h][0])[q % per] for q in range(K)] for h in range(len(hosts))]
    role = {}
    for h in range(len(hosts)):
        for k, c in enumerate(major[h]):
            role[c] = ("rank", h, k, F[h], k, 1)
        for k, c in enumerate(minor[h]):
            role[c] = ("rank", h, k, E[h], K + k, per)
        for q in range(K):
            role[F[h][q]] = ("F", h, q)
            role[E[h][q]] = ("E", h, q)
    p = {"major": major, "minor": minor, "F": F, "E": E, "role": role, "per": per}
    _CACHE["p"] = p
    return p


def _u8(view):
    return view.bitcast(dt.uint8)


def _send(g, T, topo, core, dst, sem, mask, out_c, in_c, out_x, in_x, sent):
    rid, pid = topo.addr(dst, core)
    g.remote_dma(out_ap=out_x, in_ap=in_x, remote_sem=sem, local_sem=T.sem.sent, pid=pid, routing_id=rid,
                 dma_engine_mask=mask)
    g.remote_dma(out_ap=_u8(out_c), in_ap=_u8(in_c), remote_sem=sem, local_sem=T.sem.sent, pid=pid, routing_id=rid,
                 dma_engine_mask=mask)
    sent[0] += 2 * _bits(mask)


def _send_many(g, T, topo, core, dsts, sem, mask, out_c, in_c, out_x, in_x, sent):
    ids = []
    for d in dsts:
        rid, pid = topo.addr(d, core)
        ids.append(DstId(rid=rid, pnc=pid))
    g.remote_dma_fused([RemoteDMATransfer(dst_ids=ids, dma_engine_mask=mask, remote_sem=sem, srcs=[in_x],
                                          dsts=[out_x for _ in dsts])], local_sem=T.sem.sent)
    g.remote_dma_fused([RemoteDMATransfer(dst_ids=ids, dma_engine_mask=mask, remote_sem=sem, srcs=[_u8(in_c)],
                                          dsts=[_u8(out_c) for _ in dsts])], local_sem=T.sem.sent)
    sent[0] += 2 * _bits(mask)


def _masks(topo, core, near, far):
    off = topo.mask(core, far)
    return off, topo.mask(core, near) & ~off


def _group(d):
    return d // (K // 2) if d < K else (d - K) % 2


def _sel(T, i):
    return T.idc[:, 128 * i:128 * i + 128], T.idx[:, 128 * i:128 * i + 128]


def _rank(g, core, T, topo, P, h, k, owners, d_index, n_id):
    v, t, s, sy, S = g.vector, g.tensor, g.scalar, g.sync, T.sem
    w = 256 // K
    sent = [0]
    far = [q for q in range(K) if not _same_chip(topo, owners[q], core)]
    near = [q for q in range(K) if _same_chip(topo, owners[q], core)]
    far = [q for q in far if q > near[-1]] + [q for q in far if q < near[0]]
    halves = [far[0] // 2, 1 - far[0] // 2]
    sy.dma_start(T.b_sb[:], T.b[:]).then_inc(S.ld_b, 16)
    for i in range(4):
        (s if i % 2 == 0 else sy).dma_start(T.a_sb[:, 512 * i:512 * i + 512],
                                            T.a[:, 512 * i:512 * i + 512]).then_inc(S["ld_a%d" % i], 16)
    v.memset(T.zb[:], 0.0).then_inc(S.zz, 1)
    v.wait_ge(S.zz, 1)
    v.quantize_mx(T.zq[:], T.zx[:], T.zb[:]).then_inc(S.pad, 1)
    g.wait_ge(S.pad, 1)
    full = topo.mask(core, owners[near[0]])
    for q in near:
        _send(g, T, topo, core, owners[q], S.padin, full, T.lc[:, SLOT * k + w:SLOT * k + 2 * w], T.zq[:, 0:w],
              T.lx[:, SLOT * k + w:SLOT * k + 2 * w], T.zx[:, 0:w], sent)
    v.wait_ge(S.ld_b, 16)
    v.quantize_mx(T.bq[:], T.bx[:], T.b_sb[:]).then_inc(S.qb, 1)
    t.wait_ge(S.qb, 1)
    for i in range(4):
        v.wait_ge(S["ld_a%d" % i], 16)
        v.quantize_mx(T.aq[:, 128 * i:128 * i + 128], T.ax[:, 128 * i:128 * i + 128],
                      T.a_sb[:, 512 * i:512 * i + 512]).then_inc(S["qa%d" % i], 1)
        t.wait_ge(S["qa%d" % i], 1)
        if i < 3:
            t.matmul_mx(T.ps[:, 512 * i:512 * i + 256], T.aq[:, 128 * i:128 * i + 128], T.ax[:, 128 * i:128 * i + 128],
                        T.bq[:], T.bx[:], True, True).then_inc(S["mm%d" % i], 1)
    for n, H in enumerate(halves):
        t.matmul_mx(T.ps[:, 512 * (3 + n):512 * (3 + n) + 128], T.aq[:, 384:512], T.ax[:, 384:512],
                    T.bq[:, 128 * H:128 * H + 128], T.bx[:, 128 * H:128 * H + 128],
                    True, True).then_inc(S["mm3" if n == 0 else "mm3b"], 1)
    for i in range(3):
        s.wait_ge(S["mm%d" % i], 1)
        s.activation(T.t_bf[:, i:1024:4], T.ps[:, 512 * i:512 * i + 256],
                     ActivationFunctionType.Copy).then_inc(S["cs%d" % i], 1)
    for n, H in enumerate(halves):
        v.wait_ge(S["mm3" if n == 0 else "mm3b"], 1)
        v.tensor_copy(T.t_bf[:, 512 * H + 3:512 * H + 512:4],
                      T.ps[:, 512 * (3 + n):512 * (3 + n) + 128]).then_inc(S["cs3" if n == 0 else "cs3b"], 1)
        if n == 0:
            for i in range(3):
                v.wait_ge(S["cs%d" % i], 1)
        v.wait_ge(S["cs3" if n == 0 else "cs3b"], 1)
        v.quantize_mx(T.tq[:, 128 * H:128 * H + 128], T.tx[:, 128 * H:128 * H + 128],
                      T.t_bf[:, 512 * H:512 * H + 512]).then_inc(S["tq%d" % H], 1)
    off, on = _masks(topo, core, owners[near[0]], owners[far[0]])
    seen = set()
    for q in far + near:
        if q // 2 not in seen:
            g.wait_ge(S["tq%d" % (q // 2)], 1)
            seen.add(q // 2)
        _send(g, T, topo, core, owners[q], S["l1_%d" % k], off if q in far else on,
              T.lc[:, SLOT * k:SLOT * k + w], T.tq[:, w * q:w * q + w],
              T.lx[:, SLOT * k:SLOT * k + w], T.tx[:, w * q:w * q + w], sent)
    first = _group(d_index)
    order = [first, 1 - first]
    t.wait_ge(S.idin, n_id * 2 * _bits(full))
    t.wait_ge(S.cs3b, 1)
    for n, H in enumerate(order):
        if n == 1:
            for i in range(4):
                t.wait_ge(S["cs%d" % i], 1)
        t.wait_ge(S["y%d" % H], 4 * _bits(off))
        for i in range(4):
            bank = 512 * (i + 4 * (1 - n))
            c, x = _sel(T, i)
            t.matmul_mx(T.ps[:, bank:bank + 128], c, x, T.yc[:, 128 * H:128 * H + 128],
                        T.yx[:, 128 * H:128 * H + 128], True, True).then_inc(S["u%d_%d" % (H, i)], 1)
        for i in range(4):
            bank = 512 * (i + 4 * (1 - n))
            out = T.y_sb[:, 512 * H + i:512 * H + 512:4]
            if i < 2:
                v.wait_ge(S["u%d_%d" % (H, i)], 1)
                v.tensor_copy(out, T.ps[:, bank:bank + 128]).then_inc(S["ov%d" % H], 1)
            else:
                s.wait_ge(S["u%d_%d" % (H, i)], 1)
                s.activation(out, T.ps[:, bank:bank + 128], ActivationFunctionType.Copy).then_inc(S["os%d" % H], 1)
        sy.wait_ge(S["ov%d" % H], 2)
        sy.wait_ge(S["os%d" % H], 2)
        sy.dma_start(T.y[:, 512 * H:512 * H + 512], T.y_sb[:, 512 * H:512 * H + 512]).then_inc(S["st%d" % H], 16)
    for H in order:
        sy.wait_ge(S["st%d" % H], 16)
    g.wait_ge(S.sent, sent[0])


def _add(g, T, sources, first_bank, tile, done, cv, cs):
    v, t, s, S = g.vector, g.tensor, g.scalar, T.sem
    w = 256 // K
    for n, (sem, cnt, c, x) in enumerate(sources):
        t.wait_ge(sem, cnt)
        for i in range(4):
            bank = 512 * (first_bank + i)
            ic, ix = _sel(T, i)
            mm = t.matmul_mx(T.ps[:, bank:bank + 128], ic, ix, c, x, n == 0, n == len(sources) - 1)
            if n == len(sources) - 1:
                mm.then_inc(S["%s_%d" % (done, i)], 1)
    for i in range(4):
        bank = 512 * (first_bank + i)
        if i < 2:
            v.wait_ge(S["%s_%d" % (done, i)], 1)
            v.tensor_copy(tile[:, i:4 * w:4], T.ps[:, bank:bank + w]).then_inc(cv, 1)
        else:
            s.wait_ge(S["%s_%d" % (done, i)], 1)
            s.activation(tile[:, i:4 * w:4], T.ps[:, bank:bank + w], ActivationFunctionType.Copy).then_inc(cs, 1)
    v.wait_ge(cv, 2)
    v.wait_ge(cs, 2)


def _helper(g, core, T, topo, P, kind, h, q):
    v, t, S = g.vector, g.tensor, T.sem
    w = 256 // K
    sent = [0]
    final = kind == "F"
    per = P["per"]
    my_rank = P["major"][h][q] if final else P["minor"][h][q // per]
    twin = P["F"][1 - h][q]
    off, on = _masks(topo, core, my_rank, twin)
    ne = _bits(off)
    slots = list(range(7)) if final else list(range(len(P["minor"][h])))
    v.memset(T.dg[:, 0:516], 1.0).then_inc(S.ones, 1)
    v.memset(T.zb[:], 0.0).then_inc(S.zz, 1)
    v.memset(T.pt1[:, 4 * w:512], 0.0).then_inc(S.zz, 1)
    v.memset(T.pt2[:, 4 * w:512], 0.0).then_inc(S.zz, 1)
    g.wait_ge(S.ones, 1)
    g.affine_select(T.dg[:, 0:516], T.dg[:, 0:516], [[1, 516]], AluOpType.is_equal, 0.0, -3, -4).then_inc(S.diag, 1)
    v.wait_ge(S.diag, 1)
    for i in range(4):
        c, x = _sel(T, i)
        v.quantize_mx(c, x, T.dg[:, 3 - i:515 - i]).then_inc(S.idq, 1)
    v.wait_ge(S.zz, 3)
    own = q if final else q // per
    for sl in [x for x in slots if x != own]:
        v.quantize_mx(T.lc[:, SLOT * sl + w:SLOT * sl + SLOT], T.lx[:, SLOT * sl + w:SLOT * sl + SLOT],
                      T.zb[:]).then_inc(S.pad, 1)
    g.wait_ge(S.idq, 4)
    share = 512 if final else 512 // per
    lo = 0 if final else share * (q % per)
    full = topo.mask(core, my_rank)
    _send(g, T, topo, core, my_rank, S.idin, full, T.idc[:, lo:lo + share], T.idc[:, lo:lo + share],
          T.idx[:, lo:lo + share], T.idx[:, lo:lo + share], sent)
    t.wait_ge(S.idq, 4)
    t.wait_ge(S.pad, len(slots) - 1)
    t.wait_ge(S.padin, 2 * _bits(full))

    def slot(sl):
        return T.lc[:, SLOT * sl:SLOT * sl + 128], T.lx[:, SLOT * sl:SLOT * sl + 128]

    if final:
        order = [(q - 1) % K, (q - 2) % K, q, (q - 3) % K]
    else:
        mine, other = q // per, 1 - q // per
        order = [other, mine] if q % per == 0 else [mine, other]
    _add(g, T, [(S["l1_%d" % k], 2 * ne) + slot(k) for k in order], 0, T.pt1, "p1", S.c1v, S.c1s)
    v.quantize_mx(T.pq1[:], T.px1[:], T.pt1[:]).then_inc(S.q1, 1)
    g.wait_ge(S.q1, 1)
    if not final:
        sl = K + h
        _send_many(g, T, topo, core, [P["F"][h][q], twin], S["l2_%d" % h], off,
                   T.lc[:, SLOT * sl:SLOT * sl + w], T.pq1[:, 0:w], T.lx[:, SLOT * sl:SLOT * sl + w], T.px1[:, 0:w], sent)
        g.wait_ge(S.sent, sent[0])
        return
    sl = K + 2
    _send(g, T, topo, core, twin, S.l2_2, off, T.lc[:, SLOT * sl:SLOT * sl + w], T.pq1[:, 0:w],
          T.lx[:, SLOT * sl:SLOT * sl + w], T.px1[:, 0:w], sent)
    src = [(S.q1, 1, T.pq1[:], T.px1[:])]
    for j in (h, 2, 1 - h):
        src.append((S["l2_%d" % j], 2 * ne) + slot(K + j))
    _add(g, T, src, 4, T.pt2, "p2", S.c2v, S.c2s)
    v.quantize_mx(T.pq2[:], T.px2[:], T.pt2[:]).then_inc(S.q2, 1)
    g.wait_ge(S.q2, 1)
    ranks = P["major"][h] + P["minor"][h]
    mine = _group(q)
    r1 = [c for d, c in enumerate(ranks) if _group(d) == mine and c != my_rank]
    r2 = [c for d, c in enumerate(ranks) if _group(d) != mine]
    rot = q % 2
    r1, r2 = r1[rot:] + r1[:rot], r2[rot:] + r2[:rot]
    oc, ox = T.yc[:, w * q:w * q + w], T.yx[:, w * q:w * q + w]
    _send_many(g, T, topo, core, r1, S["y%d" % mine], off, oc, T.pq2[:, 0:w], ox, T.px2[:, 0:w], sent)
    _send(g, T, topo, core, my_rank, S["y%d" % mine], on, oc, T.pq2[:, 0:w], ox, T.px2[:, 0:w], sent)
    _send_many(g, T, topo, core, r2, S["y%d" % mine], off, oc, T.pq2[:, 0:w], ox, T.px2[:, 0:w], sent)
    g.wait_ge(S.sent, sent[0])


def rank_program(g, core, T, topo):
    P = _plan(T, topo)
    r = P["role"].get(core)
    if r is None:
        return
    if r[0] == "rank":
        _rank(g, core, T, topo, P, r[1], r[2], r[3], r[4], r[5])
    else:
        _helper(g, core, T, topo, P, r[0], r[1], r[2])
